import numpy as np
import ml_dtypes


def mxq(x, axis, fmt="e4m3"):
    dtype, down = {"e4m3": (ml_dtypes.float8_e4m3fn, 7), "e5m2": (ml_dtypes.float8_e5m2, 14)}[fmt]
    v = np.moveaxis(np.asarray(x, np.float32).astype(ml_dtypes.bfloat16).astype(np.float64), axis, -1)
    blocks = v.reshape(v.shape[:-1] + (-1, 32))
    amax = np.abs(blocks).max(-1, keepdims=True)
    byte = np.maximum(np.where(amax > 0, np.frexp(amax)[1] - 1 + 127, 0) - down, 1)
    scale = np.exp2(byte - 127.0)
    codes = (blocks / scale).astype(np.float32).astype(dtype).astype(np.float64)
    return np.moveaxis((codes * scale).reshape(v.shape), -1, axis)


WIDE = False


def mx_kscale(k):
    if not WIDE:
        return np.ones(k)
    levels = np.array([30, -30])
    if k % 512:
        return np.exp2(np.random.permutation(np.resize(levels, k // 32))).repeat(32)
    a = np.empty((k // 512, 16))
    for p in range(k // 512):
        a[p, :8] = np.random.permutation(np.resize(levels, 8))
        for g in range(8):
            far = levels[np.abs(levels - a[p, g]) >= 10]
            a[p, g + 8] = far[np.random.randint(len(far))]
    return np.exp2(a.ravel()).repeat(32)


def f64(x):
    return np.asarray(x).astype(np.float64)


def striped(idx):
    return np.tile(np.asarray(idx).reshape(-1, 16).T, (8, 1)).astype(np.uint16)


def unstriped(offs):
    return offs[:16].T.reshape(-1).astype(np.int64)


E2M1 = np.array([0.0, 0.5, 1.0, 1.5, 2.0, 3.0, 4.0, 6.0, -0.0, -0.5, -1.0, -1.5, -2.0, -3.0, -4.0, -6.0])


def pack_weight(w, fmt):
    k, n = w.shape
    w = f64(np.asarray(w, np.float32).astype(ml_dtypes.bfloat16)).reshape(k // 32, 32, n)
    amax = np.abs(w).max(1)
    if fmt in ("e4m3", "e5m2"):
        byte = np.frexp(amax)[1] - 1 + 127 - (7 if fmt == "e4m3" else 14)
    else:
        mant, ex = np.frexp(amax / 6.0)
        byte = np.where(mant > 0.5, ex, ex - 1) + 127
    byte = np.clip(np.where(amax > 0, byte, 1), 1, 254)
    scaled = (w * np.exp2(127.0 - byte)[:, None, :]).reshape(k, n).astype(np.float32)
    by_word = np.ascontiguousarray(scaled.reshape(k // 512, 128, 4, n).transpose(0, 1, 3, 2))
    if fmt in ("e4m3", "e5m2"):
        words = by_word.astype(ml_dtypes.float8_e4m3fn if fmt == "e4m3" else ml_dtypes.float8_e5m2).view(np.uint8)
    else:
        c = by_word.astype(ml_dtypes.float4_e2m1fn).view(np.uint8) & 0xF
        words = (c[..., 0::2] | (c[..., 1::2] << 4)).reshape(k // 512, 128, 2 * n)
    return np.ascontiguousarray(words), np.ascontiguousarray(byte.astype(np.uint8).reshape(k // 512, 16, n))


def unpack_weight(words, scales, fmt):
    g, _, n = scales.shape
    words = np.ascontiguousarray(words).reshape(g, 128, n, -1)
    if fmt in ("e4m3", "e5m2"):
        vals = words.view(ml_dtypes.float8_e4m3fn if fmt == "e4m3" else ml_dtypes.float8_e5m2).astype(np.float64)
    else:
        nib = np.empty((g, 128, n, 4), np.uint8)
        nib[..., 0::2] = words & 0xF
        nib[..., 1::2] = words >> 4
        vals = E2M1[nib]
    vals = vals * np.repeat(np.exp2(scales.astype(np.float64) - 127.0), 8, axis=1)[..., None]
    return vals.transpose(0, 1, 3, 2).reshape(g * 512, n)


def bf(x):
    return np.asarray(x, np.float32).astype(ml_dtypes.bfloat16)


def planes(Y):
    r, m = Y.shape
    b = f64(bf(Y)).reshape(r // 32, 32, m)
    amax = np.abs(b).max(1)
    byte = np.clip(np.where(amax > 0, np.frexp(amax)[1] - 1 + 127 - 7, 1), 1, 254)
    codes = (b * np.exp2(127.0 - byte)[:, None, :]).reshape(r, m).astype(np.float32).astype(ml_dtypes.float8_e4m3fn).view(np.uint8)
    words = codes.reshape(r // 512, 128, 4, m).transpose(0, 1, 3, 2)
    return np.ascontiguousarray(words), np.ascontiguousarray(byte.astype(np.uint8).reshape(r // 512, 16, m))


K, T, J, R, N, Z = 512, 1024, 256, 512, 512, 512


def setup_inputs():
    n = np.random.standard_normal
    idx = np.random.permutation(T)[:J]
    idx2 = np.random.permutation(Z)[:J]
    fk = mx_kscale(K)
    fr = mx_kscale(R)
    wp = pack_weight(n((K, R)) * 1 / np.sqrt(K) * fk[:, None] * fr, "e2m1")
    wbp = pack_weight(n((R, N)) * 1 / np.sqrt(R) / fr[:, None], "e5m2")
    return {
        "xf": (n((K, T))).astype(np.float32),
        "fk": (np.random.uniform(0.5, 2.0, (K, 1)) / fk[:, None]).astype(np.float32),
        "w_words": wp[0],
        "w_scales": wp[1],
        "wb_words": wbp[0],
        "wb_scales": wbp[1],
        "tz": (n((N, Z)) * 0.6).astype(np.float32),
        "rw": (np.random.uniform(0.5, 2.0, (1, J))).astype(np.float32),
        "offs": striped(idx),
        "offs2": striped(idx2),
    }


def reference(xf, fk, w_words, w_scales, wb_words, wb_scales, tz, rw, offs, offs2):
    idx = unstriped(offs)
    idx2 = unstriped(offs2)
    wu = unpack_weight(w_words, w_scales, "e2m1")
    wbu = unpack_weight(wb_words, wb_scales, "e5m2")
    xg = f64(xf)[:, idx]
    x1 = np.pad(xg, ((0, 0), (1, 0)))[:, :J]
    u = (xg - 0.6 * x1) * f64(fk)
    uq = mxq(u, 0, "e4m3")
    a = wu.T @ uq
    ha = np.maximum(a, 0.0)
    h1 = np.pad(ha, ((0, 0), (2, 0)))[:, :J]
    hid = ha - 0.5 * h1
    hidq = mxq(hid, 0, "e5m2")
    p = wbu.T @ hidq
    y = np.maximum(p, f64(tz)[:, idx2]) * f64(rw)
    words, scales = planes(y)
    return y, words, scales

@@ -1,0 +1,234 @@
+from contextlib import ExitStack
+
+import concourse.mybir as mybir
+from concourse.masks import make_identity
+
+K, T, J, R, N, Z = 512, 1024, 256, 512, 512, 512
+FLOPS = 2 * K * R * J + 2 * R * N * J
+
+F32 = mybir.dt.float32
+BF16 = mybir.dt.bfloat16
+I32 = mybir.dt.int32
+U32 = mybir.dt.uint32
+U16 = mybir.dt.uint16
+U8 = mybir.dt.uint8
+E4M3 = mybir.dt.float8_e4m3fn_x4
+E5M2 = mybir.dt.float8_e5m2_x4
+E2M1 = mybir.dt.float4_e2m1fn_x4
+ALU = mybir.AluOpType
+ACT = mybir.ActivationFunctionType
+
+P = 128
+PACK = 4
+HALF = J // 2
+PAD = 8
+LIST_COLS = HALF // 16
+
+
+def interleave(copy, dst, src):
+    copy(out=dst.rearrange("p (c i t) -> p c t i", i=4, t=PACK), in_=src.rearrange("p t (c i) -> p c t i", i=4))
+
+
+def tile_list_steps_lagged_floored_pl_kernel(
+    tc, xf, fk, w_words, w_scales, wb_words, wb_scales, tz, rw, offs, offs2, out_0, out_1, out_2
+):
+    nc = tc.nc
+    with ExitStack() as ctx:
+        sb = ctx.enter_context(tc.tile_pool(name="sb", bufs=1))
+        ps = ctx.enter_context(tc.psum_pool(name="ps", bufs=1))
+
+        def tile(name, shape, dtype):
+            return sb.tile(shape, dtype, name=name, align_bytes=64)
+
+        offs_t = sb.tile([P, J // 16], U16, name="offs_t")
+        offs2_t = sb.tile([P, J // 16], U16, name="offs2_t")
+
+        x_rows = xf.rearrange("(p t) c -> p t c", t=PACK)
+        x = [tile("x%d" % t, [P, T], F32) for t in range(PACK)]
+        ws_raw = tile("ws_raw", [P, R], U8)
+        wbs_raw = tile("wbs_raw", [P, N], U8)
+        w_raw = tile("w_raw", [P, 2 * R], U8)
+        wb_raw = tile("wb_raw", [P, N], U32)
+        fk_t = tile("fk_t", [P, PACK], F32)
+        rw_t = tile("rw_t", [P, 2], F32)
+        tz_t = [tile("tz%d" % i, [P, 2, Z], F32) for i in range(2)]
+
+        tz_rows = tz.rearrange("(p t) c -> p t c", t=PACK)
+        ident = tile("ident", [P, P], F32)
+
+        def load_scales(queue, dst, src):
+            for q in range(4):
+                queue.dma_start(dst[:].bitcast(I32)[32 * q : 32 * q + 4, :], src[0].bitcast(I32)[4 * q : 4 * q + 4, :])
+
+        nc.gpsimd.memset(ws_raw[:].bitcast(U32), 0)
+        nc.vector.memset(wbs_raw[:].bitcast(U32), 0)
+        nc.sync.dma_start(offs_t[:], offs)
+        nc.sync.dma_start(fk_t[:], fk.rearrange("(p t) o -> p (t o)", t=PACK))
+        nc.sync.dma_start(x[0][:], x_rows[:, 0, :])
+        load_scales(nc.sync, ws_raw, w_scales)
+        nc.sync.dma_start(x[1][:], x_rows[:, 1, :])
+        nc.sync.dma_start(w_raw[:].bitcast(I32), w_words[0].bitcast(I32))
+        nc.sync.dma_start(x[2][:], x_rows[:, 2, :])
+        nc.sync.dma_start(x[3][:], x_rows[:, 3, :])
+        nc.sync.dma_start(wb_raw[:].bitcast(I32), wb_words[0].rearrange("p n b -> p (n b)").bitcast(I32))
+        nc.sync.dma_start(tz_t[0][:], tz_rows[:, 0:2, :])
+        nc.sync.dma_start(offs2_t[:], offs2)
+        load_scales(nc.sync, wbs_raw, wb_scales)
+        nc.sync.dma_start(tz_t[1][:], tz_rows[:, 2:4, :])
+        make_identity(nc, ident[:])
+        nc.gpsimd.dma_start(rw_t[:], rw.rearrange("o (p e) -> p (o e)", e=2))
+
+        g = tile("g", [P, PACK, PAD + J], F32)
+        ha = tile("ha", [P, PAD + PACK * J], F32)
+        nc.vector.memset(g[:, :, 0:PAD], 0.0)
+        nc.vector.memset(ha[:, 0:PAD], 0.0)
+
+        fk_wide = tile("fk_wide", [P, PACK, HALF], F32)
+        nc.scalar.activation(
+            out=fk_wide[:], in_=fk_t[:].rearrange("p (t o) -> p t o", o=1).to_broadcast([P, PACK, HALF]), func=ACT.Copy
+        )
+        rw_ps = ps.tile([P, 2, P], F32, name="rw_ps")
+
+        w_d = tile("w_d", [P, 2 * R], U8)
+        ws_d = tile("ws_d", [P, R], U8)
+        wb_d = tile("wb_d", [P, N], U32)
+        wbs_d = tile("wbs_d", [P, N], U8)
+
+        def deal(dst, src):
+            nc.vector.tensor_copy(
+                out=dst.rearrange("p (t m) -> p t m", t=PACK), in_=src.rearrange("p (m t) -> p t m", t=PACK)
+            )
+
+
+        g1 = tile("g1", [P, PACK, HALF], F32)
+        d = [tile("d%d" % h, [P, PACK, HALF], F32) for h in range(2)]
+
+        def step(h, t):
+            lo = PAD + h * HALF
+            nc.vector.scalar_tensor_tensor(
+                out=d[h][:, t, :], in0=g[:, t, lo - 1 : lo - 1 + HALF], scalar=-0.6, in1=g[:, t, lo : lo + HALF],
+                op0=ALU.mult, op1=ALU.add,
+            )
+
+        for t in range(PACK):
+            nc.vector.tensor_tensor(
+                out=g[:, t, PAD : PAD + HALF], in0=x[t][:].indirect(offs_t[:, 0:LIST_COLS]), in1=fk_wide[:, t, :],
+                op=ALU.mult,
+            )
+            nc.scalar.activation(out=g1[:, t, :], in_=x[t][:].indirect(offs_t[:, LIST_COLS:]), func=ACT.Copy)
+            nc.scalar.activation(
+                out=g[:, t, PAD + HALF :], in_=g1[:, t, :], func=ACT.Copy, scale=fk_t[:, t : t + 1]
+            )
+            step(0, t)
+            if t < PACK - 1:
+                step(1, t)
+            if t == 0:
+                deal(ws_d[:], ws_raw[:])
+            if t == 1:
+                deal(w_d[:].bitcast(U16), w_raw[:].bitcast(U16))
+
+
+        ub = [tile("ub%d" % h, [P, PACK * HALF], BF16) for h in range(2)]
+        uc = [tile("uc%d" % h, [P, HALF], U32) for h in range(2)]
+        us = [tile("us%d" % h, [P, HALF], U8) for h in range(2)]
+        a_ps = [ps.tile([P, PACK, HALF], F32, name="a_ps%d" % h) for h in range(2)]
+        hb = [tile("hb%d" % h, [P, PACK * HALF], BF16) for h in range(2)]
+        hc = [tile("hc%d" % h, [P, HALF], U32) for h in range(2)]
+        hs = [tile("hs%d" % h, [P, HALF], U8) for h in range(2)]
+        p_ps = [ps.tile([P, PACK, HALF], F32, name="p_ps%d" % h) for h in range(2)]
+        tzg = [tile("tzg%d" % h, [P, PACK, HALF], F32) for h in range(2)]
+        m = [tile("m%d" % h, [P, PACK, HALF], F32) for h in range(2)]
+        y = [tile("y%d" % h, [P, PACK, HALF], F32) for h in range(2)]
+        yb = [tile("yb%d" % h, [P, PACK * HALF], BF16) for h in range(2)]
+        yc = tile("yc", [P, J], U32)
+        ys = tile("ys", [P, J], U8)
+
+        def first_product(h):
+            nc.vector.quantize_mx(out=uc[h][:].bitcast(E4M3), scales=us[h][:], in_=ub[h][:])
+            for t in range(PACK):
+                nc.tensor.matmul_mx(
+                    out=a_ps[h][:, t, :],
+                    lhsT=w_d[:, 2 * P * t : 2 * P * (t + 1)].bitcast(E2M1),
+                    lhsT_scale=ws_d[:, P * t : P * (t + 1)],
+                    rhs=uc[h][:].bitcast(E4M3),
+                    rhs_scale=us[h][:],
+                    start=True,
+                    stop=True,
+                )
+            lo = PAD + h * PACK * HALF
+            nc.scalar.activation(
+                out=ha[:, lo : lo + PACK * HALF].rearrange("p (j t) -> p j t", t=PACK),
+                in_=a_ps[h][:].rearrange("p t j -> p j t"),
+                func=ACT.Relu,
+            )
+
+        def second_product(h):
+            lo = PAD + h * PACK * HALF
+            nc.vector.scalar_tensor_tensor(
+                out=hb[h][:], in0=ha[:, lo - 2 * PACK : lo - 2 * PACK + PACK * HALF], scalar=-0.5,
+                in1=ha[:, lo : lo + PACK * HALF], op0=ALU.mult, op1=ALU.add,
+            )
+            nc.vector.quantize_mx(out=hc[h][:].bitcast(E5M2), scales=hs[h][:], in_=hb[h][:])
+            for t in range(PACK):
+                nc.tensor.matmul_mx(
+                    out=p_ps[h][:, t, :],
+                    lhsT=wb_d[:, P * t : P * (t + 1)].bitcast(E5M2),
+                    lhsT_scale=wbs_d[:, P * t : P * (t + 1)],
+                    rhs=hc[h][:].bitcast(E5M2),
+                    rhs_scale=hs[h][:],
+                    start=True,
+                    stop=True,
+                )
+
+        def gather_floor(h):
+            for t in range(PACK):
+                nc.scalar.activation(
+                    out=tzg[h][:, t, :],
+                    in_=tz_t[t // 2][:, t % 2, :].indirect(offs2_t[:, h * LIST_COLS : (h + 1) * LIST_COLS]),
+                    func=ACT.Copy,
+                )
+
+        y_rows = out_0.rearrange("(p t) j -> p t j", t=PACK)
+        words_out = out_1[0].rearrange("p c b -> p (c b)").bitcast(I32)
+
+        def result(h):
+            cols = slice(h * HALF, (h + 1) * HALF)
+            nc.vector.tensor_tensor(out=m[h][:], in0=p_ps[h][:], in1=tzg[h][:], op=ALU.max)
+            nc.vector.tensor_tensor(
+                out=y[h][:].rearrange("p t (n e) -> p t n e", e=2),
+                in0=m[h][:].rearrange("p t (n e) -> p t n e", e=2),
+                in1=rw_ps[:, :, h * HALF // 2 : (h + 1) * HALF // 2]
+                .rearrange("p (o e) n -> p o n e", o=1)
+                .to_broadcast([P, PACK, HALF // 2, 2]),
+                op=ALU.mult,
+            )
+            nc.sync.dma_start(y_rows[:, :, cols], y[h][:])
+
+        def planes(h, copy):
+            cols = slice(h * HALF, (h + 1) * HALF)
+            interleave(copy, yb[h][:], y[h][:])
+            nc.vector.quantize_mx(out=yc[:, cols].bitcast(E4M3), scales=ys[:, cols], in_=yb[h][:])
+            nc.sync.dma_start(words_out[:, cols], yc[:, cols].bitcast(I32))
+
+        interleave(nc.vector.tensor_copy, ub[0][:], d[0][:])
+        step(1, PACK - 1)
+        first_product(0)
+        interleave(nc.scalar.copy, ub[1][:], d[1][:])
+        first_product(1)
+        for e in range(2):
+            nc.tensor.transpose(rw_ps[:, e, :], rw_t[:, e : e + 1].to_broadcast([P, P]), ident[:])
+        deal(wb_d[:], wb_raw[:])
+        deal(wbs_d[:], wbs_raw[:])
+        second_product(0)
+        gather_floor(0)
+        second_product(1)
+        gather_floor(1)
+        result(0)
+        result(1)
+        planes(0, nc.scalar.copy)
+        planes(1, nc.vector.tensor_copy)
+        for q in range(4):
+            queue = nc.sync if q % 2 == 0 else nc.scalar
+            queue.dma_start(
+                out_2[0].bitcast(I32)[4 * q : 4 * q + 4, :], ys[:].bitcast(I32)[32 * q : 32 * q + 4, :]
+            )

@@ -37,8 +37,8 @@ def tile_list_steps_lagged_floored_pl_kernel(
         sb = ctx.enter_context(tc.tile_pool(name="sb", bufs=1))
         ps = ctx.enter_context(tc.psum_pool(name="ps", bufs=1))
 
-        def tile(name, shape, dtype):
-            return sb.tile(shape, dtype, name=name, align_bytes=64)
+        def tile(name, shape, dtype, tag=""):
+            return sb.tile(shape, dtype, name=name, tag=tag or name, align_bytes=64)
 
         offs_t = sb.tile([P, J // 16], U16, name="offs_t")
         offs2_t = sb.tile([P, J // 16], U16, name="offs2_t")
@@ -71,28 +71,24 @@ def tile_list_steps_lagged_floored_pl_kernel(
         nc.sync.dma_start(x[2][:], x_rows[:, 2, :])
         nc.sync.dma_start(x[3][:], x_rows[:, 3, :])
         nc.sync.dma_start(wb_raw[:].bitcast(I32), wb_words[0].rearrange("p n b -> p (n b)").bitcast(I32))
-        nc.sync.dma_start(tz_t[0][:], tz_rows[:, 0:2, :])
-        nc.sync.dma_start(offs2_t[:], offs2)
         load_scales(nc.sync, wbs_raw, wb_scales)
+        nc.sync.dma_start(offs2_t[:], offs2)
+        nc.sync.dma_start(tz_t[0][:], tz_rows[:, 0:2, :])
         nc.sync.dma_start(tz_t[1][:], tz_rows[:, 2:4, :])
         make_identity(nc, ident[:])
         nc.gpsimd.dma_start(rw_t[:], rw.rearrange("o (p e) -> p (o e)", e=2))
 
         g = tile("g", [P, PACK, PAD + J], F32)
-        ha = tile("ha", [P, PAD + PACK * J], F32)
         nc.vector.memset(g[:, :, 0:PAD], 0.0)
-        nc.vector.memset(ha[:, 0:PAD], 0.0)
 
-        fk_wide = tile("fk_wide", [P, PACK, HALF], F32)
-        nc.scalar.activation(
-            out=fk_wide[:], in_=fk_t[:].rearrange("p (t o) -> p t o", o=1).to_broadcast([P, PACK, HALF]), func=ACT.Copy
-        )
+        fk_wide = {t: tile("fk_wide%d" % t, [P, HALF], F32) for t in (0, 2, 3)}
+        for t in fk_wide:
+            nc.scalar.activation(out=fk_wide[t][:], in_=fk_t[:, t : t + 1].to_broadcast([P, HALF]), func=ACT.Copy)
         rw_ps = ps.tile([P, 2, P], F32, name="rw_ps")
 
         w_d = tile("w_d", [P, 2 * R], U8)
         ws_d = tile("ws_d", [P, R], U8)
         wb_d = tile("wb_d", [P, N], U32)
-        wbs_d = tile("wbs_d", [P, N], U8)
 
         def deal(dst, src):
             nc.vector.tensor_copy(
@@ -100,44 +96,49 @@ def tile_list_steps_lagged_floored_pl_kernel(
             )
 
 
-        g1 = tile("g1", [P, PACK, HALF], F32)
-        d = [tile("d%d" % h, [P, PACK, HALF], F32) for h in range(2)]
+        raw = tile("raw", [P, PACK, J], F32)
+        d = tile("d", [P, PACK, J], F32)
 
-        def step(h, t):
-            lo = PAD + h * HALF
-            nc.vector.scalar_tensor_tensor(
-                out=d[h][:, t, :], in0=g[:, t, lo - 1 : lo - 1 + HALF], scalar=-0.6, in1=g[:, t, lo : lo + HALF],
-                op0=ALU.mult, op1=ALU.add,
-            )
+        def gather_on_scalar(t, lo):
+            nc.scalar.activation(out=raw[:, t, lo:], in_=x[t][:].indirect(offs_t[:, lo // 16 :]), func=ACT.Copy)
+            nc.scalar.activation(out=g[:, t, PAD + lo :], in_=raw[:, t, lo:], func=ACT.Copy, scale=fk_t[:, t : t + 1])
 
-        for t in range(PACK):
+        def gather_on_vector(t):
             nc.vector.tensor_tensor(
-                out=g[:, t, PAD : PAD + HALF], in0=x[t][:].indirect(offs_t[:, 0:LIST_COLS]), in1=fk_wide[:, t, :],
+                out=g[:, t, PAD : PAD + HALF], in0=x[t][:].indirect(offs_t[:, 0:LIST_COLS]), in1=fk_wide[t][:],
                 op=ALU.mult,
             )
-            nc.scalar.activation(out=g1[:, t, :], in_=x[t][:].indirect(offs_t[:, LIST_COLS:]), func=ACT.Copy)
-            nc.scalar.activation(
-                out=g[:, t, PAD + HALF :], in_=g1[:, t, :], func=ACT.Copy, scale=fk_t[:, t : t + 1]
+
+        def step(out, t, lo, width):
+            nc.vector.scalar_tensor_tensor(
+                out=out, in0=g[:, t, PAD + lo - 1 : PAD + lo - 1 + width], scalar=-0.6,
+                in1=g[:, t, PAD + lo : PAD + lo + width], op0=ALU.mult, op1=ALU.add,
             )
-            step(0, t)
-            if t < PACK - 1:
-                step(1, t)
-            if t == 0:
-                deal(ws_d[:], ws_raw[:])
-            if t == 1:
-                deal(w_d[:].bitcast(U16), w_raw[:].bitcast(U16))
 
-
+        gather_on_vector(0)
+        gather_on_scalar(0, HALF)
+        step(d[:, 0, :], 0, 0, J)
+        gather_on_scalar(1, 0)
+        deal(ws_d[:], ws_raw[:])
+        deal(w_d[:].bitcast(U16), w_raw[:].bitcast(U16))
+        step(d[:, 1, :], 1, 0, J)
+        gather_on_vector(2)
+        gather_on_scalar(2, HALF)
+        step(d[:, 2, :], 2, 0, J)
+        gather_on_vector(3)
+        gather_on_scalar(3, HALF)
+        for h in range(2):
+            step(d[:, 3, h * HALF : (h + 1) * HALF], 3, h * HALF, HALF)
         ub = [tile("ub%d" % h, [P, PACK * HALF], BF16) for h in range(2)]
+        for h in range(2):
+            interleave(nc.vector.tensor_copy, ub[h][:], d[:, :, h * HALF : (h + 1) * HALF])
+
         uc = [tile("uc%d" % h, [P, HALF], U32) for h in range(2)]
         us = [tile("us%d" % h, [P, HALF], U8) for h in range(2)]
         a_ps = [ps.tile([P, PACK, HALF], F32, name="a_ps%d" % h) for h in range(2)]
-        hb = [tile("hb%d" % h, [P, PACK * HALF], BF16) for h in range(2)]
         hc = [tile("hc%d" % h, [P, HALF], U32) for h in range(2)]
         hs = [tile("hs%d" % h, [P, HALF], U8) for h in range(2)]
-        p_ps = [ps.tile([P, PACK, HALF], F32, name="p_ps%d" % h) for h in range(2)]
-        tzg = [tile("tzg%d" % h, [P, PACK, HALF], F32) for h in range(2)]
-        m = [tile("m%d" % h, [P, PACK, HALF], F32) for h in range(2)]
+        p_ps = [[ps.tile([P, 2, HALF], F32, name="p_ps%d%d" % (h, i)) for i in range(2)] for h in range(2)]
         y = [tile("y%d" % h, [P, PACK, HALF], F32) for h in range(2)]
         yb = [tile("yb%d" % h, [P, PACK * HALF], BF16) for h in range(2)]
         yc = tile("yc", [P, J], U32)
@@ -165,13 +166,13 @@ def tile_list_steps_lagged_floored_pl_kernel(
         def second_product(h):
             lo = PAD + h * PACK * HALF
             nc.vector.scalar_tensor_tensor(
-                out=hb[h][:], in0=ha[:, lo - 2 * PACK : lo - 2 * PACK + PACK * HALF], scalar=-0.5,
+                out=hb[h], in0=ha[:, lo - 2 * PACK : lo - 2 * PACK + PACK * HALF], scalar=-0.5,
                 in1=ha[:, lo : lo + PACK * HALF], op0=ALU.mult, op1=ALU.add,
             )
-            nc.vector.quantize_mx(out=hc[h][:].bitcast(E5M2), scales=hs[h][:], in_=hb[h][:])
+            nc.vector.quantize_mx(out=hc[h][:].bitcast(E5M2), scales=hs[h][:], in_=hb[h])
             for t in range(PACK):
                 nc.tensor.matmul_mx(
-                    out=p_ps[h][:, t, :],
+                    out=p_ps[h][t // 2][:, t % 2, :],
                     lhsT=wb_d[:, P * t : P * (t + 1)].bitcast(E5M2),
                     lhsT_scale=wbs_d[:, P * t : P * (t + 1)],
                     rhs=hc[h][:].bitcast(E5M2),
@@ -180,55 +181,90 @@ def tile_list_steps_lagged_floored_pl_kernel(
                     stop=True,
                 )
 
-        def gather_floor(h):
-            for t in range(PACK):
+        def gather_floor(dst, i, lo, width):
+            for e in range(2):
                 nc.scalar.activation(
-                    out=tzg[h][:, t, :],
-                    in_=tz_t[t // 2][:, t % 2, :].indirect(offs2_t[:, h * LIST_COLS : (h + 1) * LIST_COLS]),
+                    out=dst[:, e, lo : lo + width],
+                    in_=tz_t[i][:, e, :].indirect(offs2_t[:, lo // 16 : (lo + width) // 16]),
                     func=ACT.Copy,
                 )
 
         y_rows = out_0.rearrange("(p t) j -> p t j", t=PACK)
         words_out = out_1[0].rearrange("p c b -> p (c b)").bitcast(I32)
 
-        def result(h):
-            cols = slice(h * HALF, (h + 1) * HALF)
-            nc.vector.tensor_tensor(out=m[h][:], in0=p_ps[h][:], in1=tzg[h][:], op=ALU.max)
+        def floor(h, pairs):
+            for i in range(2):
+                nc.vector.tensor_tensor(
+                    out=pairs[i], in0=p_ps[h][i][:], in1=tzg[i][:, :, h * HALF : (h + 1) * HALF],
+                    op=ALU.max,
+                )
+
+        def weigh(h, rows, lo, width, floored):
+            count = rows.stop - rows.start
+            first = (h * HALF + lo) // 2
             nc.vector.tensor_tensor(
-                out=y[h][:].rearrange("p t (n e) -> p t n e", e=2),
-                in0=m[h][:].rearrange("p t (n e) -> p t n e", e=2),
-                in1=rw_ps[:, :, h * HALF // 2 : (h + 1) * HALF // 2]
+                out=y[h][:, rows, lo : lo + width].rearrange("p t (n e) -> p t n e", e=2),
+                in0=floored.rearrange("p t (n e) -> p t n e", e=2),
+                in1=rw_ps[:, :, first : first + width // 2]
                 .rearrange("p (o e) n -> p o n e", o=1)
-                .to_broadcast([P, PACK, HALF // 2, 2]),
+                .to_broadcast([P, count, width // 2, 2]),
                 op=ALU.mult,
             )
+
+        def round_result(h, lo, width):
+            interleave(nc.scalar.copy, yb[h][:, PACK * lo : PACK * (lo + width)], y[h][:, :, lo : lo + width])
+
+        def quantise_result(h, lo, width):
+            cols = slice(h * HALF + lo, h * HALF + lo + width)
+            nc.vector.quantize_mx(
+                out=yc[:, cols].bitcast(E4M3), scales=ys[:, cols], in_=yb[h][:, PACK * lo : PACK * (lo + width)]
+            )
+
+        def store(h):
+            cols = slice(h * HALF, (h + 1) * HALF)
             nc.sync.dma_start(y_rows[:, :, cols], y[h][:])
 
-        def planes(h, copy):
+        def store_words(h):
             cols = slice(h * HALF, (h + 1) * HALF)
-            interleave(copy, yb[h][:], y[h][:])
-            nc.vector.quantize_mx(out=yc[:, cols].bitcast(E4M3), scales=ys[:, cols], in_=yb[h][:])
             nc.sync.dma_start(words_out[:, cols], yc[:, cols].bitcast(I32))
 
-        interleave(nc.vector.tensor_copy, ub[0][:], d[0][:])
-        step(1, PACK - 1)
+        tzg = [tile("tzg0", [P, 2, J], F32)]
+        gather_floor(tzg[0], 0, 0, J)
+        ha = tile("ha", [P, PAD + PACK * J], F32, tag="tz0")
         first_product(0)
-        interleave(nc.scalar.copy, ub[1][:], d[1][:])
         first_product(1)
         for e in range(2):
             nc.tensor.transpose(rw_ps[:, e, :], rw_t[:, e : e + 1].to_broadcast([P, P]), ident[:])
+        nc.vector.memset(ha[:, 0:PAD], 0.0)
         deal(wb_d[:], wb_raw[:])
+        wbs_d = tile("wbs_d", [P, N], U8)
         deal(wbs_d[:], wbs_raw[:])
+        h_bf = tile("h_bf", [P, PACK * J], BF16, tag="wbs_raw")
+        hb = [h_bf[:, h * PACK * HALF : (h + 1) * PACK * HALF] for h in range(2)]
         second_product(0)
-        gather_floor(0)
         second_product(1)
-        gather_floor(1)
-        result(0)
-        result(1)
-        planes(0, nc.scalar.copy)
-        planes(1, nc.vector.tensor_copy)
+        tzg.append(tile("tzg1", [P, 2, J], F32, tag="tz0"))
+        gather_floor(tzg[1], 1, 0, HALF)
+        gather_floor(tzg[1], 1, HALF, HALF)
+        m0 = [tile("m0%d" % i, [P, 2, HALF], F32) for i in range(2)]
+        floor(0, [m0[0][:], m0[1][:]])
+        for i in range(2):
+            weigh(0, slice(2 * i, 2 * i + 2), 0, HALF, m0[i][:])
+        store(0)
+        round_result(0, 0, HALF)
+        m1 = tile("m1", [P, PACK, HALF], F32, tag="m00")
+        floor(1, [m1[:, 0:2, :], m1[:, 2:4, :]])
+        quantise_result(0, 0, HALF)
+        store_words(0)
+        for lo in (0, HALF // 2):
+            weigh(1, slice(0, PACK), lo, HALF // 2, m1[:, :, lo : lo + HALF // 2])
+            round_result(1, lo, HALF // 2)
+        store(1)
+        for lo in (0, HALF // 2):
+            quantise_result(1, lo, HALF // 2)
+        store_words(1)
         for q in range(4):
-            queue = nc.sync if q % 2 == 0 else nc.scalar
+            queue = nc.scalar if q % 2 == 0 else nc.sync
             queue.dma_start(
                 out_2[0].bitcast(I32)[4 * q : 4 * q + 4, :], ys[:].bitcast(I32)[32 * q : 32 * q + 4, :]
             )

@@ -21,6 +21,7 @@ ACT = mybir.ActivationFunctionType
 P = 128
 PACK = 4
 HALF = J // 2
+QUARTER = J // 4
 PAD = 8
 LIST_COLS = HALF // 16
 
@@ -61,9 +62,9 @@ def tile_list_steps_lagged_floored_pl_kernel(
                 queue.dma_start(dst[:].bitcast(I32)[32 * q : 32 * q + 4, :], src[0].bitcast(I32)[4 * q : 4 * q + 4, :])
 
         nc.gpsimd.memset(ws_raw[:].bitcast(U32), 0)
-        nc.vector.memset(wbs_raw[:].bitcast(U32), 0)
+        nc.gpsimd.memset(wbs_raw[:].bitcast(U32), 0)
         nc.sync.dma_start(offs_t[:], offs)
-        nc.sync.dma_start(fk_t[:], fk.rearrange("(p t) o -> p (t o)", t=PACK))
+        nc.scalar.dma_start(fk_t[:], fk.rearrange("(p t) o -> p (t o)", t=PACK))
         nc.sync.dma_start(x[0][:], x_rows[:, 0, :])
         load_scales(nc.sync, ws_raw, w_scales)
         nc.sync.dma_start(x[1][:], x_rows[:, 1, :])
@@ -71,12 +72,12 @@ def tile_list_steps_lagged_floored_pl_kernel(
         nc.sync.dma_start(x[2][:], x_rows[:, 2, :])
         nc.sync.dma_start(x[3][:], x_rows[:, 3, :])
         nc.sync.dma_start(wb_raw[:].bitcast(I32), wb_words[0].rearrange("p n b -> p (n b)").bitcast(I32))
-        load_scales(nc.sync, wbs_raw, wb_scales)
         nc.sync.dma_start(offs2_t[:], offs2)
+        nc.sync.dma_start(rw_t[:], rw.rearrange("o (p e) -> p (o e)", e=2))
         nc.sync.dma_start(tz_t[0][:], tz_rows[:, 0:2, :])
         nc.sync.dma_start(tz_t[1][:], tz_rows[:, 2:4, :])
         make_identity(nc, ident[:])
-        nc.gpsimd.dma_start(rw_t[:], rw.rearrange("o (p e) -> p (o e)", e=2))
+        load_scales(nc.gpsimd, wbs_raw, wb_scales)
 
         g = tile("g", [P, PACK, PAD + J], F32)
         nc.vector.memset(g[:, :, 0:PAD], 0.0)
@@ -156,19 +157,23 @@ def tile_list_steps_lagged_floored_pl_kernel(
                     start=True,
                     stop=True,
                 )
-            lo = PAD + h * PACK * HALF
-            nc.scalar.activation(
-                out=ha[:, lo : lo + PACK * HALF].rearrange("p (j t) -> p j t", t=PACK),
-                in_=a_ps[h][:].rearrange("p t j -> p j t"),
-                func=ACT.Relu,
+            for j in (0, QUARTER):
+                lo = PAD + PACK * (h * HALF + j)
+                nc.scalar.activation(
+                    out=ha[:, lo : lo + PACK * QUARTER].rearrange("p (j t) -> p j t", t=PACK),
+                    in_=a_ps[h][:, :, j : j + QUARTER].rearrange("p t j -> p j t"),
+                    func=ACT.Relu,
+                )
+
+        def lag(quarter):
+            lo = quarter * PACK * QUARTER
+            hi = lo + PACK * QUARTER
+            nc.vector.scalar_tensor_tensor(
+                out=h_bf[:, lo:hi], in0=ha[:, lo:hi], scalar=-0.5, in1=ha[:, PAD + lo : PAD + hi],
+                op0=ALU.mult, op1=ALU.add,
             )
 
         def second_product(h):
-            lo = PAD + h * PACK * HALF
-            nc.vector.scalar_tensor_tensor(
-                out=hb[h], in0=ha[:, lo - 2 * PACK : lo - 2 * PACK + PACK * HALF], scalar=-0.5,
-                in1=ha[:, lo : lo + PACK * HALF], op0=ALU.mult, op1=ALU.add,
-            )
             nc.vector.quantize_mx(out=hc[h][:].bitcast(E5M2), scales=hs[h][:], in_=hb[h])
             for t in range(PACK):
                 nc.tensor.matmul_mx(
@@ -241,7 +246,10 @@ def tile_list_steps_lagged_floored_pl_kernel(
         deal(wbs_d[:], wbs_raw[:])
         h_bf = tile("h_bf", [P, PACK * J], BF16, tag="wbs_raw")
         hb = [h_bf[:, h * PACK * HALF : (h + 1) * PACK * HALF] for h in range(2)]
+        for quarter in range(3):
+            lag(quarter)
         second_product(0)
+        lag(3)
         second_product(1)
         tzg.append(tile("tzg1", [P, 2, J], F32, tag="tz0"))
         gather_floor(tzg[1], 1, 0, HALF)

@@ -62,22 +62,22 @@ def tile_list_steps_lagged_floored_pl_kernel(
                 queue.dma_start(dst[:].bitcast(I32)[32 * q : 32 * q + 4, :], src[0].bitcast(I32)[4 * q : 4 * q + 4, :])
 
         nc.gpsimd.memset(ws_raw[:].bitcast(U32), 0)
-        nc.gpsimd.memset(wbs_raw[:].bitcast(U32), 0)
+        nc.vector.memset(wbs_raw[:].bitcast(U32), 0)
         nc.sync.dma_start(offs_t[:], offs)
-        nc.scalar.dma_start(fk_t[:], fk.rearrange("(p t) o -> p (t o)", t=PACK))
+        nc.sync.dma_start(fk_t[:], fk.rearrange("(p t) o -> p (t o)", t=PACK))
         nc.sync.dma_start(x[0][:], x_rows[:, 0, :])
         load_scales(nc.sync, ws_raw, w_scales)
         nc.sync.dma_start(x[1][:], x_rows[:, 1, :])
         nc.sync.dma_start(w_raw[:].bitcast(I32), w_words[0].bitcast(I32))
         nc.sync.dma_start(x[2][:], x_rows[:, 2, :])
         nc.sync.dma_start(x[3][:], x_rows[:, 3, :])
-        nc.sync.dma_start(wb_raw[:].bitcast(I32), wb_words[0].rearrange("p n b -> p (n b)").bitcast(I32))
         nc.sync.dma_start(offs2_t[:], offs2)
-        nc.sync.dma_start(rw_t[:], rw.rearrange("o (p e) -> p (o e)", e=2))
         nc.sync.dma_start(tz_t[0][:], tz_rows[:, 0:2, :])
+        nc.sync.dma_start(wb_raw[:].bitcast(I32), wb_words[0].rearrange("p n b -> p (n b)").bitcast(I32))
+        load_scales(nc.sync, wbs_raw, wb_scales)
         nc.sync.dma_start(tz_t[1][:], tz_rows[:, 2:4, :])
         make_identity(nc, ident[:])
-        load_scales(nc.gpsimd, wbs_raw, wb_scales)
+        nc.gpsimd.dma_start(rw_t[:], rw.rearrange("o (p e) -> p (o e)", e=2))
 
         g = tile("g", [P, PACK, PAD + J], F32)
         nc.vector.memset(g[:, :, 0:PAD], 0.0)

from contextlib import ExitStack

import concourse.mybir as mybir
from concourse.masks import make_identity

K, T, J, R, N, Z = 512, 1024, 256, 512, 512, 512
FLOPS = 2 * K * R * J + 2 * R * N * J

F32 = mybir.dt.float32
BF16 = mybir.dt.bfloat16
I32 = mybir.dt.int32
U32 = mybir.dt.uint32
U16 = mybir.dt.uint16
U8 = mybir.dt.uint8
E4M3 = mybir.dt.float8_e4m3fn_x4
E5M2 = mybir.dt.float8_e5m2_x4
E2M1 = mybir.dt.float4_e2m1fn_x4
ALU = mybir.AluOpType
ACT = mybir.ActivationFunctionType

P = 128
PACK = 4
HALF = J // 2
QUARTER = J // 4
PAD = 8
LIST_COLS = HALF // 16


def interleave(copy, dst, src):
    copy(out=dst.rearrange("p (c i t) -> p c t i", i=4, t=PACK), in_=src.rearrange("p t (c i) -> p c t i", i=4))


def tile_list_steps_lagged_floored_pl_kernel(
    tc, xf, fk, w_words, w_scales, wb_words, wb_scales, tz, rw, offs, offs2, out_0, out_1, out_2
):
    nc = tc.nc
    with ExitStack() as ctx:
        sb = ctx.enter_context(tc.tile_pool(name="sb", bufs=1))
        ps = ctx.enter_context(tc.psum_pool(name="ps", bufs=1))

        def tile(name, shape, dtype, tag=""):
            return sb.tile(shape, dtype, name=name, tag=tag or name, align_bytes=64)

        offs_t = sb.tile([P, J // 16], U16, name="offs_t")
        offs2_t = sb.tile([P, J // 16], U16, name="offs2_t")

        x_rows = xf.rearrange("(p t) c -> p t c", t=PACK)
        x = [tile("x%d" % t, [P, T], F32) for t in range(PACK)]
        ws_raw = tile("ws_raw", [P, R], U8)
        wbs_raw = tile("wbs_raw", [P, N], U8)
        w_raw = tile("w_raw", [P, 2 * R], U8)
        wb_raw = tile("wb_raw", [P, N], U32)
        fk_t = tile("fk_t", [P, PACK], F32)
        rw_t = tile("rw_t", [P, 2], F32)
        tz_t = [tile("tz%d" % i, [P, 2, Z], F32) for i in range(2)]

        tz_rows = tz.rearrange("(p t) c -> p t c", t=PACK)
        ident = tile("ident", [P, P], F32)

        def load_scales(queue, dst, src):
            for q in range(4):
                queue.dma_start(dst[:].bitcast(I32)[32 * q : 32 * q + 4, :], src[0].bitcast(I32)[4 * q : 4 * q + 4, :])

        nc.gpsimd.memset(ws_raw[:].bitcast(U32), 0)
        nc.vector.memset(wbs_raw[:].bitcast(U32), 0)
        nc.sync.dma_start(offs_t[:], offs)
        nc.sync.dma_start(fk_t[:], fk.rearrange("(p t) o -> p (t o)", t=PACK))
        nc.sync.dma_start(x[0][:], x_rows[:, 0, :])
        load_scales(nc.sync, ws_raw, w_scales)
        nc.sync.dma_start(x[1][:], x_rows[:, 1, :])
        nc.sync.dma_start(w_raw[:].bitcast(I32), w_words[0].bitcast(I32))
        nc.sync.dma_start(x[2][:], x_rows[:, 2, :])
        nc.sync.dma_start(x[3][:], x_rows[:, 3, :])
        nc.sync.dma_start(offs2_t[:], offs2)
        nc.sync.dma_start(tz_t[0][:], tz_rows[:, 0:2, :])
        nc.sync.dma_start(wb_raw[:].bitcast(I32), wb_words[0].rearrange("p n b -> p (n b)").bitcast(I32))
        load_scales(nc.sync, wbs_raw, wb_scales)
        nc.sync.dma_start(tz_t[1][:], tz_rows[:, 2:4, :])
        make_identity(nc, ident[:])
        nc.gpsimd.dma_start(rw_t[:], rw.rearrange("o (p e) -> p (o e)", e=2))

        g = tile("g", [P, PACK, PAD + J], F32)
        nc.vector.memset(g[:, :, 0:PAD], 0.0)

        fk_wide = {t: tile("fk_wide%d" % t, [P, HALF], F32) for t in (0, 2, 3)}
        for t in fk_wide:
            nc.scalar.activation(out=fk_wide[t][:], in_=fk_t[:, t : t + 1].to_broadcast([P, HALF]), func=ACT.Copy)
        rw_ps = ps.tile([P, 2, P], F32, name="rw_ps")

        w_d = tile("w_d", [P, 2 * R], U8)
        ws_d = tile("ws_d", [P, R], U8)
        wb_d = tile("wb_d", [P, N], U32)

        def deal(dst, src):
            nc.vector.tensor_copy(
                out=dst.rearrange("p (t m) -> p t m", t=PACK), in_=src.rearrange("p (m t) -> p t m", t=PACK)
            )


        raw = tile("raw", [P, PACK, J], F32)
        d = tile("d", [P, PACK, J], F32)

        def gather_on_scalar(t, lo):
            nc.scalar.activation(out=raw[:, t, lo:], in_=x[t][:].indirect(offs_t[:, lo // 16 :]), func=ACT.Copy)
            nc.scalar.activation(out=g[:, t, PAD + lo :], in_=raw[:, t, lo:], func=ACT.Copy, scale=fk_t[:, t : t + 1])

        def gather_on_vector(t):
            nc.vector.tensor_tensor(
                out=g[:, t, PAD : PAD + HALF], in0=x[t][:].indirect(offs_t[:, 0:LIST_COLS]), in1=fk_wide[t][:],
                op=ALU.mult,
            )

        def step(out, t, lo, width):
            nc.vector.scalar_tensor_tensor(
                out=out, in0=g[:, t, PAD + lo - 1 : PAD + lo - 1 + width], scalar=-0.6,
                in1=g[:, t, PAD + lo : PAD + lo + width], op0=ALU.mult, op1=ALU.add,
            )

        gather_on_vector(0)
        gather_on_scalar(0, HALF)
        step(d[:, 0, :], 0, 0, J)
        gather_on_scalar(1, 0)
        deal(ws_d[:], ws_raw[:])
        deal(w_d[:].bitcast(U16), w_raw[:].bitcast(U16))
        step(d[:, 1, :], 1, 0, J)
        gather_on_vector(2)
        gather_on_scalar(2, HALF)
        step(d[:, 2, :], 2, 0, J)
        gather_on_vector(3)
        gather_on_scalar(3, HALF)
        for h in range(2):
            step(d[:, 3, h * HALF : (h + 1) * HALF], 3, h * HALF, HALF)
        ub = [tile("ub%d" % h, [P, PACK * HALF], BF16) for h in range(2)]
        for h in range(2):
            interleave(nc.vector.tensor_copy, ub[h][:], d[:, :, h * HALF : (h + 1) * HALF])

        uc = [tile("uc%d" % h, [P, HALF], U32) for h in range(2)]
        us = [tile("us%d" % h, [P, HALF], U8) for h in range(2)]
        a_ps = [ps.tile([P, PACK, HALF], F32, name="a_ps%d" % h) for h in range(2)]
        hc = [tile("hc%d" % h, [P, HALF], U32) for h in range(2)]
        hs = [tile("hs%d" % h, [P, HALF], U8) for h in range(2)]
        p_ps = [[ps.tile([P, 2, HALF], F32, name="p_ps%d%d" % (h, i)) for i in range(2)] for h in range(2)]
        y = [tile("y%d" % h, [P, PACK, HALF], F32) for h in range(2)]
        yb = [tile("yb%d" % h, [P, PACK * HALF], BF16) for h in range(2)]
        yc = tile("yc", [P, J], U32)
        ys = tile("ys", [P, J], U8)

        def first_product(h):
            nc.vector.quantize_mx(out=uc[h][:].bitcast(E4M3), scales=us[h][:], in_=ub[h][:])
            for t in range(PACK):
                nc.tensor.matmul_mx(
                    out=a_ps[h][:, t, :],
                    lhsT=w_d[:, 2 * P * t : 2 * P * (t + 1)].bitcast(E2M1),
                    lhsT_scale=ws_d[:, P * t : P * (t + 1)],
                    rhs=uc[h][:].bitcast(E4M3),
                    rhs_scale=us[h][:],
                    start=True,
                    stop=True,
                )
            for j in (0, QUARTER):
                lo = PAD + PACK * (h * HALF + j)
                nc.scalar.activation(
                    out=ha[:, lo : lo + PACK * QUARTER].rearrange("p (j t) -> p j t", t=PACK),
                    in_=a_ps[h][:, :, j : j + QUARTER].rearrange("p t j -> p j t"),
                    func=ACT.Relu,
                )

        def lag(quarter):
            lo = quarter * PACK * QUARTER
            hi = lo + PACK * QUARTER
            nc.vector.scalar_tensor_tensor(
                out=h_bf[:, lo:hi], in0=ha[:, lo:hi], scalar=-0.5, in1=ha[:, PAD + lo : PAD + hi],
                op0=ALU.mult, op1=ALU.add,
            )

        def second_product(h):
            nc.vector.quantize_mx(out=hc[h][:].bitcast(E5M2), scales=hs[h][:], in_=hb[h])
            for t in range(PACK):
                nc.tensor.matmul_mx(
                    out=p_ps[h][t // 2][:, t % 2, :],
                    lhsT=wb_d[:, P * t : P * (t + 1)].bitcast(E5M2),
                    lhsT_scale=wbs_d[:, P * t : P * (t + 1)],
                    rhs=hc[h][:].bitcast(E5M2),
                    rhs_scale=hs[h][:],
                    start=True,
                    stop=True,
                )

        def gather_floor(dst, i, lo, width):
            for e in range(2):
                nc.scalar.activation(
                    out=dst[:, e, lo : lo + width],
                    in_=tz_t[i][:, e, :].indirect(offs2_t[:, lo // 16 : (lo + width) // 16]),
                    func=ACT.Copy,
                )

        y_rows = out_0.rearrange("(p t) j -> p t j", t=PACK)
        words_out = out_1[0].rearrange("p c b -> p (c b)").bitcast(I32)

        def floor(h, pairs):
            for i in range(2):
                nc.vector.tensor_tensor(
                    out=pairs[i], in0=p_ps[h][i][:], in1=tzg[i][:, :, h * HALF : (h + 1) * HALF],
                    op=ALU.max,
                )

        def weigh(h, rows, lo, width, floored):
            count = rows.stop - rows.start
            first = (h * HALF + lo) // 2
            nc.vector.tensor_tensor(
                out=y[h][:, rows, lo : lo + width].rearrange("p t (n e) -> p t n e", e=2),
                in0=floored.rearrange("p t (n e) -> p t n e", e=2),
                in1=rw_ps[:, :, first : first + width // 2]
                .rearrange("p (o e) n -> p o n e", o=1)
                .to_broadcast([P, count, width // 2, 2]),
                op=ALU.mult,
            )

        def round_result(h, lo, width):
            interleave(nc.scalar.copy, yb[h][:, PACK * lo : PACK * (lo + width)], y[h][:, :, lo : lo + width])

        def quantise_result(h, lo, width):
            cols = slice(h * HALF + lo, h * HALF + lo + width)
            nc.vector.quantize_mx(
                out=yc[:, cols].bitcast(E4M3), scales=ys[:, cols], in_=yb[h][:, PACK * lo : PACK * (lo + width)]
            )

        def store(h):
            cols = slice(h * HALF, (h + 1) * HALF)
            nc.sync.dma_start(y_rows[:, :, cols], y[h][:])

        def store_words(h):
            cols = slice(h * HALF, (h + 1) * HALF)
            nc.sync.dma_start(words_out[:, cols], yc[:, cols].bitcast(I32))

        tzg = [tile("tzg0", [P, 2, J], F32)]
        gather_floor(tzg[0], 0, 0, J)
        ha = tile("ha", [P, PAD + PACK * J], F32, tag="tz0")
        first_product(0)
        first_product(1)
        for e in range(2):
            nc.tensor.transpose(rw_ps[:, e, :], rw_t[:, e : e + 1].to_broadcast([P, P]), ident[:])
        nc.vector.memset(ha[:, 0:PAD], 0.0)
        deal(wb_d[:], wb_raw[:])
        wbs_d = tile("wbs_d", [P, N], U8)
        deal(wbs_d[:], wbs_raw[:])
        h_bf = tile("h_bf", [P, PACK * J], BF16, tag="wbs_raw")
        hb = [h_bf[:, h * PACK * HALF : (h + 1) * PACK * HALF] for h in range(2)]
        for quarter in range(3):
            lag(quarter)
        second_product(0)
        lag(3)
        second_product(1)
        tzg.append(tile("tzg1", [P, 2, J], F32, tag="tz0"))
        gather_floor(tzg[1], 1, 0, HALF)
        gather_floor(tzg[1], 1, HALF, HALF)
        m0 = [tile("m0%d" % i, [P, 2, HALF], F32) for i in range(2)]
        floor(0, [m0[0][:], m0[1][:]])
        for i in range(2):
            weigh(0, slice(2 * i, 2 * i + 2), 0, HALF, m0[i][:])
        store(0)
        round_result(0, 0, HALF)
        m1 = tile("m1", [P, PACK, HALF], F32, tag="m00")
        floor(1, [m1[:, 0:2, :], m1[:, 2:4, :]])
        quantise_result(0, 0, HALF)
        store_words(0)
        for lo in (0, HALF // 2):
            weigh(1, slice(0, PACK), lo, HALF // 2, m1[:, :, lo : lo + HALF // 2])
            round_result(1, lo, HALF // 2)
        store(1)
        for lo in (0, HALF // 2):
            quantise_result(1, lo, HALF // 2)
        store_words(1)
        for q in range(4):
            queue = nc.scalar if q % 2 == 0 else nc.sync
            queue.dma_start(
                out_2[0].bitcast(I32)[4 * q : 4 * q + 4, :], ys[:].bitcast(I32)[32 * q : 32 * q + 4, :]
            )
